import numpy as np, ml_dtypes
CORES = [16,17,18,19,32,33,34,35]
N = 8
BF = ml_dtypes.bfloat16
def gentries(a):
    return np.ascontiguousarray(a.reshape(8, 16, -1).transpose(0, 2, 1)).reshape(8, -1)
def gtable(e):
    e = np.asarray(e); return np.ascontiguousarray(e.reshape(8, -1, 16).transpose(0, 2, 1)).reshape(128, -1).astype(np.int32)
S, R, B, C, P, STEPS, O = 2560, 1792, 64, 4, 2, 2, 448
def pick(t, l):
    return np.stack([np.stack([np.take(t[r, g], l[r, g], axis=1) for g in range(8)]) for r in range(N)])
def widen(t, send):
    s = pick(t, send)
    return np.stack([np.concatenate([t[r]] + [s[(r + 1 + m) % N][:, :, (N - 2 - m) * B:(N - 1 - m) * B] for m in range(N - 1)], axis=2) for r in range(N)])
def groups(a):
    return np.stack([gentries(v) for v in a])
def first(v):
    u, i, n = np.unique(v, return_index=True, return_inverse=True); return i[n.reshape(-1)]
def network(rng, pairs):
    reac = np.zeros((N, 8, 2 * R), np.int64); cons = np.full((N, 8, C * S), R + O); sp = np.zeros((N, 8, O), np.int64); rx = np.zeros((N, 8, O), np.int64)
    for g in range(8):
        inc, use = [], []
        for r in range(N):
            if pairs:
                inc.append((rng.permutation(R)[:, None] + R * np.arange(2)).reshape(-1)); use.append((rng.permutation(S)[:, None] + S * np.arange(C)).reshape(-1)[:2 * R])
            else:
                inc.append(rng.permutation(2 * R)); use.append(rng.permutation(C * S)[:2 * R])
            e, u = inc[r], use[r]
            rx[r, g] = e[:O] % R; sp[r, g] = u[:O] % S
            reac[r, g, e[O:]] = u[O:] % S; cons[r, g, u[O:]] = e[O:] % R
        for r in range(N):
            for m in range(N - 1):
                q, k = (r + 1 + m) % N, N - 2 - m
                e = inc[r][m * B:(m + 1) * B]; u = use[q][k * B:(k + 1) * B]; n = np.arange(B); j = n if pairs else rng.permutation(B)
                reac[r, g, e] = S + m * B + (first(u % S) if pairs else j)
                cons[q, g, u[j]] = R + k * B + (first(e % R) if pairs else n)
    prod = rng.integers(0, R + O, (N, 8, P * S)); prod[rng.random(prod.shape) < 0.25] = R + O
    return reac, cons, prod, sp, rx
def pack(x, rate, net):
    return dict([("x", np.ascontiguousarray(np.reshape(x, (N, 128, S))).astype(np.int32)), ("rate", rate.astype(np.int32))] + [(n, np.stack([gtable(e) for e in v])) for n, v in zip(("reac", "cons", "prod", "spsend", "rxsend"), net)])
def some(rng):
    return rng.integers(0, 256, (N, 8, 16, S)) >> rng.integers(0, 8, (N, 8, 16, S)), rng.integers(1, 128, (N, 8, R)) >> rng.integers(0, 4, (N, 8, R))
def setup_inputs(rng):
    net = network(rng, False); x, k = some(rng); return pack(x, k, net)
def setup_inputs_ties(rng):
    net = network(rng, False); n = np.sum(net[1].reshape(N, 8, C, S) != R + O, axis=2)[:, :, None]
    x = np.where(n < 2, 5 + rng.integers(0, 4, (N, 8, 16, S)), 3 * n - rng.integers(0, 2, (N, 8, 16, S)))
    return pack(x, rng.integers(123, 128, (N, 8, R)), net)
def setup_inputs_twins(rng):
    net = network(rng, True); x, k = some(rng); return pack(x, k, net)
def setup_inputs_ends(rng):
    net = network(rng, False); p = rng.choice(np.array([0, R - 1, R, R + O - 1, R + O]), (N, 8, P * S))
    x = 255 * (rng.random((N, 8, 16, S)) < 0.9); k = 127 * (rng.random((N, 8, R)) < 0.9)
    return pack(x, k, net[:2] + (p,) + net[3:])
def setup_inputs_spread(rng):
    net = network(rng, False); w = rng.random((N, 8, 1, S)); x = rng.integers(0, 256, (N, 8, 16, S))
    x = np.where(w < 0.05, 0, np.where(w < 0.15, 255, np.where(w < 0.5, x, x >> 5)))
    w = rng.random((N, 8, R)); k = rng.integers(0, 128, (N, 8, R)); k = np.where(w < 0.05, 0, np.where(w < 0.15, 127, np.where(w < 0.5, k, k >> 4)))
    return pack(x, k, net)
def check_inputs(d):
    try:
        top = {"x": 255, "rate": 127, "reac": S + O - 1, "cons": R + O, "prod": R + O, "spsend": S - 1, "rxsend": R - 1}
        bad = [n + " range" for n in top if d[n].min() < 0 or d[n].max() > top[n]]
        if bad: return bad
        ra, co, ss, rs = groups(d["reac"]), groups(d["cons"]), groups(d["spsend"]), groups(d["rxsend"])
        ids = np.broadcast_to(np.arange(N * S, dtype=np.int64).reshape(N, 1, 1, S), (N, 8, 1, S)); idr = np.broadcast_to(np.arange(N * R, dtype=np.int64).reshape(N, 1, 1, R), (N, 8, 1, R))
        net = np.arange(8, dtype=np.int64).reshape(1, 8, 1); own = np.arange(N, dtype=np.int64).reshape(N, 1, 1)
        a = (net * (N * S) + pick(widen(ids, ss), ra)[:, :, 0]) * (N * R) + own * R + np.arange(2 * R) % R
        w = pick(np.concatenate([widen(idr, rs), np.full((N, 8, 1, 1), -1)], axis=3), co)[:, :, 0]
        b = ((net * (N * S) + own * S + np.arange(C * S) % S) * (N * R) + w)[w >= 0]
        return [] if np.array_equal(np.sort(a.reshape(-1)), np.sort(b)) else ["cons fits reac"]
    except Exception:
        return ["form"]
def reference(x, rate, reac, cons, prod, spsend, rxsend):
    n = x.astype(np.int32).reshape(N, 8, 16, S); k = rate.astype(np.int32)[:, :, None]; none = np.zeros((N, 8, 16, 1), np.int32)
    ra, co, pr, ss, rs = groups(reac), groups(cons), groups(prod), groups(spsend), groups(rxsend)
    for step in range(STEPS):
        a = pick(widen(n, ss), ra)
        f = np.minimum(3, (k * a[..., :R] * a[..., R:]) >> 10)
        w = np.concatenate([widen(f, rs), none], axis=3)
        demand = np.sum(pick(w, co).reshape(N, 8, 16, C, S), axis=3)
        veto = (demand > n).astype(np.int32)
        b = pick(widen(veto, ss), ra)
        f = f * ((b[..., :R] + b[..., R:]) == 0)
        w = np.concatenate([widen(f, rs), none], axis=3)
        n = n - np.sum(pick(w, co).reshape(N, 8, 16, C, S), axis=3) + np.sum(pick(w, pr).reshape(N, 8, 16, P, S), axis=3)
    return {"y": n.reshape(N, 128, S).astype(np.float32)}

@@ -1,0 +1,374 @@
+from concourse.bass import DstId, RemoteDMATransfer
+from concourse.mybir import AluOpType, ActivationFunctionType
+
+S, R, B, O = 2560, 1792, 64, 448
+OFF = 130.0
+HW = 2256
+CS = [512, 512, 512, 512, 384, 128]
+CR = [512, 512, 384, 256, 128]
+
+SCRATCH = {
+    "XI": ("sbuf", [128, S], "int32"), "RAW": ("sbuf", [128, 1184], "int32"), "SR": ("sbuf", [128, 56], "int32"),
+    "RT": ("sbuf", [128, O], "int32"), "CW": ("sbuf", [128, S + 8], "int32"),
+    "L16": ("sbuf", [128, 1184], "uint16"), "SR16": ("sbuf", [128, 56], "uint16"), "O16": ("sbuf", [128, 112], "uint16"),
+    "LS16": ("sbuf", [128, 224], "uint16"), "LF": ("sbuf", [128, 224], "float32"),
+    "LO": ("sbuf", [128, 56], "int32"), "HI": ("sbuf", [128, 56], "int32"), "LM": ("sbuf", [128, 56], "int32"),
+    "PI": ("sbuf", [128, 56], "int32"), "PN": ("sbuf", [128, 8], "int32"), "PH": ("sbuf", [128, 8], "int32"),
+    "M": ("sbuf", [128, 8], "float32"), "GT": ("sbuf", [128, 1792], "float32"), "TT": ("sbuf", [128, 1792], "float32"),
+    "Z": ("sbuf", [128, 512], "bfloat16"), "ID": ("sbuf", [128, 384], "bfloat16"), "SEL": ("sbuf", [128, 512], "bfloat16"),
+    "RB": ("sbuf", [128, O], "bfloat16"), "K": ("sbuf", [128, R], "bfloat16"), "KS": ("sbuf", [128, O], "bfloat16"),
+    "X1": ("sbuf", [128, S + O], "bfloat16"), "X2": ("sbuf", [128, S + O], "float32"),
+    "HF": ("sbuf", [128, 4 * HW], "bfloat16"), "E": ("sbuf", [128, 2 * (S + O)], "bfloat16"),
+    "SB": ("sbuf", [128, 7 * O], "bfloat16"), "XS2": ("sbuf", [128, O], "float32"),
+    "PL": ("sbuf", [128, 6 * S], "bfloat16"), "PS": ("sbuf", [128, 6 * O], "bfloat16"),
+    "U": ("sbuf", [128, O + R], "float32"), "PP": ("sbuf", [128, O + R], "float32"), "A1": ("sbuf", [128, O + R], "bfloat16"),
+    "YB": ("sbuf", [128, S], "float32"), "ACC": ("psum", [128, 4096], "float32"),
+}
+SEMAPHORES = (["cV", "cS", "cP", "cG", "sent", "stored", "dsp", "drx", "drate", "dreac", "dlist", "dcr", "dcs"]
+              + ["dx%d" % i for i in range(3)] + ["arr%d" % i for i in range(8)])
+XC = [0, 1024, 2048, 2560]
+
+ORDER = {
+    "A": ("u0s u03 u04 p0s u00 u01 u02 p03 p01 p00 p02 p04 h02", "a0s a01 h0s a03 a00 a04 a02 h03 h01 h00 h04"),
+    "B": ("g1s g0s g24 g25 g30 e0s g33 g34 g35 g21 g22 g12 g03 g04 e02 e00 e01 e03 e05 e04",
+          "g2s g3s g00 g01 g02 g15 g20 g31 g32 g05 g10 g11 g13 g23 g14"),
+    "C": ("g0s g11 e0s g10 g03 e01 e00 e02 e03 e04", "g1s g00 g01 g12 g02 g13 g14 g04"),
+    "D": ("g3s g4s g5s g31 g32 g33 e0s g14 g15 g20 g41 g42 g43 g51 g52 g53 g54 g24 g25 g30 e01 e02 e03 e00 e04 e05",
+          "g0s g1s g2s g10 g11 g12 g13 g21 g22 g23 g01 g02 g03 g00 g34 g50 g40 g04 g05 g44 g45 g55 g35"),
+    "Z": ("g20 g21 g30 g31 g41 g42 g05 g10 g11 g02 g03 e00 e01 g43 g14 g15 e03 g54 g55 e02 g24 e05 e04",
+          "g33 g34 g35 g40 g00 g01 g50 g51 g12 g13 g52 g53 g23 g22 g32 g44 g45 g04 g25"),
+}
+SCHED = {k: [[(u[0], int(u[1]), -1 if u[2] == "s" else int(u[2])) for u in q.split()] for q in v] for k, v in ORDER.items()}
+
+
+def spans(chunks):
+    out, a = {-1: (0, O)}, 0
+    for c, n in enumerate(chunks):
+        out[c] = (a, a + n)
+        a += n
+    return out
+
+
+def calls_of(seq, sp):
+    out, top = [], max(sp)
+    for w, p, c in seq:
+        n = sp[c][1] - sp[c][0]
+        if out and out[-1][0] == w and out[-1][2] + n <= 4096:
+            _, us, m = out[-1]
+            p1, c1 = us[-1]
+            if c < 0 or c1 < 0:
+                join = c == c1 and p == p1 + 1
+            elif w in "ep":
+                join = c == c1 + 1 and m == 512 * len(us)
+            else:
+                join = (p, c) == ((p1, c1 + 1) if c1 < top else (p1 + 1, 0))
+            if join:
+                out[-1] = (w, us + [(p, c)], m + n)
+                continue
+        out.append((w, [(p, c)], n))
+    return out
+
+
+def needs(call, planes, direct):
+    w, us, _ = call
+    if w == "e":
+        return [("m", p, c) for p in range(planes) for _, c in us]
+    if w == "p":
+        return [(v, 0, c) for v in "mu" for _, c in us]
+    if w == "q":
+        return [("u", 0, c) for _, c in us]
+    if w == "h":
+        return [("q" if c in direct else "p", 0, c) for _, c in us]
+    return []
+
+
+def plan(seqs, chunks, planes):
+    sp = spans(chunks)
+    direct = set(c for s in seqs for w, _, c in s if w == "q")
+    cl = [calls_of(s, sp) for s in seqs]
+    at, free, done, pe, order = [0, 0], [0.0, 0.0], {}, 0.0, []
+    while at[0] < len(cl[0]) or at[1] < len(cl[1]):
+        best = None
+        for e in (0, 1):
+            if at[e] < len(cl[e]):
+                k = cl[e][at[e]]
+                nd = needs(k, planes, direct)
+                if all(d in done for d in nd):
+                    t = max([free[e]] + [done[d] + 170 for d in nd]) + (55, 70)[e] + k[2] * (1.56 if k[0] in "gauq" else 1.0)
+                    if best is None or t < best[0]:
+                        best = (t, e, k)
+        t, e, k = best
+        free[e] = t
+        at[e] += 1
+        for p, c in k[1]:
+            done[(k[0], p, c)] = t
+            if k[0] in "ga":
+                pe = max(pe, t + 170) + 60 + 0.5 * (sp[c][1] - sp[c][0])
+                done[("m", p, c)] = pe
+                order.append((p, c))
+    return order
+
+
+def shares(core, T, topo):
+    far = [c for c in T.cores if topo.chip(c) != topo.chip(core)]
+    near = [c for c in T.cores if c != core and c not in far]
+    used = topo.engines(core, far[0])
+    out = {}
+    for group, pool in ((far, used), (near, [e for e in topo.engines(core, near[0]) if e not in used])):
+        left = list(pool)
+        for i, d in enumerate(group):
+            n = 1
+            while 2 * n + (len(group) - i - 1) * (len(pool) // len(group)) <= len(left):
+                n *= 2
+            out[d] = left[:n]
+            left = left[n:]
+    return out
+
+
+def rank_program(g, core, T, topo):
+    rank = T.rank_of(core)
+    if rank is None:
+        return
+    A, F = AluOpType, ActivationFunctionType
+    N = len(T.cores)
+    V, Sc, P, Y = g.vector, g.scalar, g.tensor, g.sync
+    queue = {"V": V, "S": Sc, "P": P, "G": g, "Y": Y}
+    ops = {e: [] for e in queue}
+    where = {}
+
+    def add(e, name, fn, deps=(), sem=None):
+        ops[e].append((name, fn, list(deps), sem))
+
+    def dma(e, out, in_, sem, deps=()):
+        add(e, None, lambda: queue[e].dma_start(out, in_), deps, sem)
+
+    mine = shares(core, T, topo)
+    arrive = sum(len(shares(c, T, topo)[core]) for c in T.cores if c != core)
+    sent = sum(len(v) for v in mine.values())
+
+    def send(rnd, src, s0, dst, d0, dep):
+        tr = []
+        for m in range(N - 1):
+            d = T.cores[(rank + 1 + m) % N]
+            rid, pid, _ = topo.addr(d)
+            k = N - 2 - m
+            tr.append(RemoteDMATransfer(dst_ids=[DstId(rid=rid, pnc=pid)], dma_engine_mask=sum(1 << e for e in mine[d]),
+                                        remote_sem=T.sem["arr%d" % rnd], src=src[:, s0 + m * B:s0 + (m + 1) * B],
+                                        dst=dst[:, d0 + k * B:d0 + (k + 1) * B]))
+        add("G", None, lambda: g.remote_dma_fused(tr, local_sem=T.sem.sent), [dep], "none")
+
+    def vop(name, fn, deps=()):
+        add("V", name, fn, deps)
+
+    dma("S", T.SR[:, 0:28], T.spsend[:], "dsp")
+    for i in range(3):
+        dma("Y", T.XI[:, XC[i]:XC[i + 1]], T.x[:, XC[i]:XC[i + 1]], "dx%d" % i)
+    dma("S", T.SR[:, 28:56], T.rxsend[:], "drx")
+    dma("S", T.RT[0:32, :], T.rate[:], "drate")
+    for c in range(2):
+        dma("Y", T.CW[6 + c:128:16, 8:8 + R], T.reac[:, c * 112:(c + 1) * 112], "dcr", ["cw0"])
+    dma("Y", T.RAW[:, 0:224], T.reac[:], "dreac")
+    for c in range(6):
+        src = T.cons[:, c * 160:(c + 1) * 160] if c < 4 else T.prod[:, (c - 4) * 160:(c - 3) * 160]
+        dma("Y", T.CW[c:128:16, 8:8 + S], src, "dcs")
+    dma("Y", T.RAW[:, 224:864], T.cons[:], "dlist")
+    dma("Y", T.RAW[:, 864:1184], T.prod[:], "dlist")
+
+    vop("z", lambda: V.memset(T.Z[:], 0.0))
+    vop("cw0", lambda: V.memset(T.CW[:], 0))
+    vop("none", lambda: V.memset(T.HF[:, R + O:4 * HW:HW], OFF))
+    add("G", "pn", lambda: g.iota(T.PN[:, 0:1], [[0, 1]], 0, 1))
+    add("G", "sel", lambda: g.affine_select(T.SEL[0:32, :], T.Z[0:32, :], [[-1, 4], [-4, 8], [0, 16]], A.not_equal, 1.0, 0, 1), ["z"])
+    for i, v in enumerate((1.0, -1.0, -16384.0)):
+        add("G", "id%d" % i, lambda i=i, v=v: g.affine_select(T.ID[:, i * 128:(i + 1) * 128], T.Z[:, 0:128], [[-1, 128]], A.not_equal, v, 0, 1), ["z"])
+    PLUS, MINUS, BIG = T.ID[:, 0:128], T.ID[:, 128:256], T.ID[:, 256:384]
+    vop("ph", lambda: V.tensor_scalar(T.PH[:, 0:1], T.PN[:, 0:1], 4, 1, A.arith_shift_right, A.bitwise_and), ["pn"])
+    vop("sr16", lambda: V.tensor_copy(T.SR16[:], T.SR[:]), [("dsp", 16), ("drx", 16)])
+    vop("lo", lambda: V.tensor_scalar(T.LO[:], T.SR[:], 15, None, A.bitwise_and))
+    vop("hi", lambda: V.tensor_scalar(T.HI[:], T.SR[:], 4, None, A.arith_shift_right))
+    vop("m1", lambda: V.tensor_copy(T.M[:, 1:2], T.PH[:, 0:1]), ["ph"])
+    vop("m0", lambda: V.tensor_scalar(T.M[:, 0:1], T.PH[:, 0:1], -1.0, 1.0, A.mult, A.add))
+    vop("lm0", lambda: V.tensor_scalar(T.LM[:, 0:28], T.LO[:, 0:28], 160.0, 8.0, A.mult, A.add), ["lo"])
+    vop("lm1", lambda: V.tensor_scalar(T.LM[:, 28:56], T.LO[:, 28:56], 112.0, 8.0, A.mult, A.add))
+    vop("rb", lambda: V.tensor_copy(T.RB[0:32, :], T.RT[0:32, :]), [("drate", 16)])
+    vop("pi", lambda: V.tensor_tensor(T.PI[:], T.LM[:], T.HI[:], A.add), ["lm1", "hi"])
+    vop("x0", lambda: V.tensor_copy(T.X1[:, XC[0]:XC[1]], T.XI[:, XC[0]:XC[1]]), [("dx0", 16)])
+    for h in range(2):
+        vop("o%d" % h, lambda h=h: V.tensor_scalar(T.O16[:, h:112:2], T.PI[:], T.M[:, h:h + 1], None, A.mult), ["pi", "m0", "m1"])
+    vop("x1", lambda: V.tensor_copy(T.X1[:, XC[1]:XC[2]], T.XI[:, XC[1]:XC[2]]), [("dx1", 16)])
+    vop("xs", lambda: V.tensor_copy(T.SB[:, 0:O], T.XI[:, 0:S].indirect(T.SR16[:, 0:28])), [("dx2", 16), "sr16"])
+    send(0, T.SB, 0, T.X1, S, "xs")
+    vop("x2", lambda: V.tensor_copy(T.X1[:, XC[2]:XC[3]], T.XI[:, XC[2]:XC[3]]))
+
+    for r in range(4):
+        add("P", "km%d" % r, lambda r=r: P.matmul(T.ACC[:, r * 512:r * 512 + O], T.SEL[0:32, r * 128:(r + 1) * 128], T.RB[0:32, :], True, True), ["sel", "rb"])
+    for r in range(4):
+        add("S", "k%d" % r, lambda r=r: Sc.activation(T.K[:, r * O:(r + 1) * O], T.ACC[:, r * 512:r * 512 + O], F.Identity, scale=1.0 / 1024), ["km%d" % r])
+    add("S", "ks", lambda: Sc.activation(T.KS[:], T.K[:, 0:R].indirect(T.SR16[:, 28:56]), F.Identity), ["k3", "sr16"])
+
+    def compose(tag, half, sem, part):
+        a, b = half * 896, (half + 1) * 896
+        cs = range(0, 6) if half == 0 else range(6, 8)
+        if part == 0:
+            vop(tag + "g", lambda: V.tensor_copy(T.GT[:, a:b], T.CW[:, 0:S + 8].indirect(T.O16[:, half * 56:(half + 1) * 56])), ["o0", "o1"] + sem)
+        elif part == 1:
+            vop(tag + "t", lambda: V.transpose(T.TT[:, a:b], T.GT[:, a:b]), [tag + "g"])
+        elif part == 2:
+            for c in cs:
+                vop(tag + "a%d" % c, lambda c=c: V.tensor_tensor(T.LF[:, c * 28:(c + 1) * 28], T.TT[:, a + c:b:32], T.TT[:, a + 16 + c:b:32], A.add), [tag + "t"])
+        else:
+            vop(tag, lambda: V.tensor_copy(T.LS16[:, cs[0] * 28:(cs[-1] + 1) * 28], T.LF[:, cs[0] * 28:(cs[-1] + 1) * 28]), [tag + "a%d" % cs[-1]])
+
+    vop("lr", lambda: V.tensor_copy(T.L16[:, 0:224], T.RAW[:, 0:224]), [("dreac", 16)])
+    for part in range(4):
+        compose("cr", 1, [("dcr", 32), ("dcs", 96)], part)
+        compose("cs", 0, [], part)
+
+    def last(e):
+        return [o[0] for o in ops[e] if o[0] is not None][-1]
+
+    def bank(c, n):
+        return T.ACC[:, (c + 1) * 512:(c + 1) * 512 + n]
+
+    def phase(kind, step, key):
+        ph = "%s%d" % (kind, step)
+        rnd = 4 * step + "ABCD".index(kind)
+        chunks = CR if kind in "AC" else CS
+        W = R if kind in "AC" else S
+        planes = {"A": 1, "B": 4, "C": 2, "D": 6}[kind]
+        sp = spans(chunks)
+        seqs = SCHED[key]
+        direct = set(c for s in seqs for w, _, c in s if w == "q")
+        X = T.X1 if step == 0 else T.X2
+        XS = T.SB[:, 0:O] if step == 0 else T.XS2[:]
+        h0, f0, e0 = step * HW, (2 + step) * HW, step * (S + O)
+        hs, es, fs = (1 + 3 * step) * O, (2 + 3 * step) * O, (3 + 3 * step) * O
+        win = {"A": X[:, 0:S + O], "B": T.HF[:, h0:h0 + R + O + 1], "C": T.E[:, e0:e0 + S + O], "D": T.HF[:, f0:f0 + R + O + 1]}[kind]
+        gate = [last("V"), last("S"), ("arr%d" % rnd, arrive)]
+        maker, sign, stores = {}, {}, []
+
+        def src(p, c, n):
+            if c < 0:
+                b = (168 if kind in "AC" else 0) + p * 28
+                return win.indirect(T.LS16[:, b:b + n // 16])
+            b = (0 if kind in "AC" else 224) + (p * W + sp[c][0]) // 16
+            return win.indirect(T.L16[:, b:b + n // 16])
+
+        def plane(p, c, n):
+            return T.PS[:, p * O:p * O + n] if c < 0 else T.PL[:, p * W + sp[c][0]:p * W + sp[c][0] + n]
+
+        def col(buf, c, n):
+            return buf[:, 0:O] if c < 0 else buf[:, O + sp[c][0]:O + sp[c][0] + n]
+
+        def own(buf, base, sbuf, c, n):
+            return sbuf if c < 0 else buf[:, base + sp[c][0]:base + sp[c][0] + n]
+
+        def make(e, w, p, c, n):
+            if w == "g":
+                o, i = plane(p, c, n), src(p, c, n)
+                if e == "V":
+                    if kind == "B":
+                        return lambda: V.tensor_scalar(o, i, OFF + 3, OFF + 3, A.min, A.subtract)
+                    return lambda: V.tensor_scalar(o, i, 12.0 if kind == "C" else OFF, None, A.is_lt if kind == "C" else A.subtract)
+                if kind == "D":
+                    return lambda: Sc.activation(o, i, F.Identity, bias=-OFF)
+                return lambda: Sc.activation(o, i, F.Relu, bias=OFF + 3 if kind == "B" else 12.0, scale=-1.0)
+            if w == "e":
+                if kind == "C":
+                    o = own(T.HF, f0, T.SB[:, fs:fs + O], c, n)
+                    return lambda: V.tensor_scalar(o, bank(c, n), OFF, OFF + 3, A.max, A.min)
+                if kind == "B":
+                    o = own(T.E, e0, T.SB[:, es:es + O], c, n)
+                else:
+                    o = own(T.X2 if step == 0 else T.YB, 0, T.XS2[:], c, n)
+                return lambda: V.tensor_tensor(o, bank(c, n), own(X, 0, XS, c, n), A.add)
+            if w == "u":
+                return lambda: V.tensor_tensor(col(T.U, c, n), src(1, c, n), own(T.K, 0, T.KS[:], c, n), A.mult)
+            if w == "q":
+                return lambda: V.tensor_tensor(col(T.PP, c, n), src(0, c, n), col(T.U, c, n), A.mult)
+            if w == "p":
+                return lambda: V.tensor_tensor(col(T.PP, c, n), bank(c, n), col(T.U, c, n), A.mult)
+            if w == "a":
+                return lambda: Sc.activation(col(T.A1, c, n), src(0, c, n), F.Identity)
+            o = own(T.HF, h0, T.SB[:, hs:hs + O], c, n)
+            shift = OFF - 1023.0 / 2048
+            if e == "V":
+                return lambda: V.tensor_scalar(o, col(T.PP, c, n), shift, None, A.add)
+            return lambda: Sc.activation(o, col(T.PP, c, n), F.Identity, bias=shift)
+
+        cl = {"V": calls_of(seqs[0], sp), "S": calls_of(seqs[1], sp)}
+        for e in "VS":
+            for w, us, n in cl[e]:
+                for p, c in us:
+                    maker[(w, p, c)] = "%s%s%d_%d" % (ph, w, us[0][0], us[0][1])
+                    if w == "g":
+                        sign[(p, c)] = e
+                if w == "e":
+                    stores.append((maker[(w,) + us[0]], sp[us[0][1]][0], n))
+        seen = {}
+        if kind == "C":
+            for c in [-1] + list(range(len(chunks))):
+                n = sp[c][1] - sp[c][0]
+                add("P", "%sf%d" % (ph, c), lambda c=c, n=n: P.matmul(bank(c, n), PLUS, own(T.HF, h0, T.SB[:, hs:hs + O], c, n), True, False), gate[:2])
+        for p, c in plan(seqs, chunks, planes):
+            n = sp[c][1] - sp[c][0]
+            seen[c] = seen.get(c, 0) + 1
+            if kind == "A":
+                lhs, rhs, dep = PLUS, col(T.A1, c, n), maker[("a", p, c)]
+            else:
+                rhs, dep = plane(p, c, n), maker[("g", p, c)]
+                lhs = BIG if kind == "C" else (MINUS if (sign[(p, c)] == "V" if kind == "B" else p < 4) else PLUS)
+            maker[("m", p, c)] = "%sm%d_%d" % (ph, p, c)
+            add("P", maker[("m", p, c)], lambda c=c, n=n, lhs=lhs, rhs=rhs, a=(seen[c] == 1 and kind != "C"), z=(seen[c] == planes):
+                P.matmul(bank(c, n), lhs, rhs, a, z), [dep, "id2"])
+        for e in "VS":
+            for k in cl[e]:
+                add(e, maker[(k[0],) + k[1][0]], make(e, k[0], k[1][0][0], k[1][0][1], k[2]), gate + [maker[d] for d in needs(k, planes, direct)])
+        out = maker.get(("h" if kind == "A" else "e", 0, -1))
+        if out is not None:
+            if kind == "D":
+                send(rnd + 1, T.XS2, 0, T.X2, S, out)
+            elif kind == "B":
+                send(rnd + 1, T.SB, es, T.E, e0 + S, out)
+            else:
+                send(rnd + 1, T.SB, hs if kind == "A" else fs, T.HF, (h0 if kind == "A" else f0) + R, out)
+        return stores
+
+    for step in range(2):
+        phase("A", step, "A")
+        if step == 0:
+            vop("ll", lambda: V.tensor_copy(T.L16[:, 224:1184], T.RAW[:, 224:1184]), [("dlist", 32)])
+        phase("B", step, "B")
+        phase("C", step, "C")
+        stores = phase("D", step, "D" if step == 0 else "Z")
+    for name, a, n in stores:
+        dma("Y", T.y[:, a:a + n], T.YB[:, a:a + n], "stored", [name])
+
+    total = {}
+    for e in "VSPG":
+        n = 0
+        for name, _, _, sem in ops[e]:
+            if sem is None:
+                n += 1
+                where[name] = ("c" + e, n)
+        total[e] = n
+    for e in queue:
+        got = {}
+        for name, fn, deps, sem in ops[e]:
+            want = {}
+            for d in deps:
+                s, v = where[d] if d in where else d
+                want[s] = max(want.get(s, 0), v)
+            for s, v in want.items():
+                if got.get(s, 0) < v:
+                    queue[e].wait_ge(T.sem[s], v)
+                    got[s] = v
+            ins = fn()
+            if sem is None:
+                ins.then_inc(T.sem["c" + e], 1)
+            elif sem != "none":
+                ins.then_inc(T.sem[sem], 16)
+    for e in "VSPG":
+        g.wait_ge(T.sem["c" + e], total[e])
+    g.wait_ge(T.sem.sent, 8 * sent)
+    Y.wait_ge(T.sem.stored, 16 * len(stores))

@@ -3,110 +3,61 @@ from concourse.mybir import AluOpType, ActivationFunctionType
 
 S, R, B, O = 2560, 1792, 64, 448
 OFF = 130.0
+BIG = 16384.0
 HW = 2256
-CS = [512, 512, 512, 512, 384, 128]
-CR = [512, 512, 384, 256, 128]
+CS = [512, 512, 256, 512, 512, 256]
+CR = [512, 512, 384, 128, 256]
+BANKS_A = [3, 4, 5, 6, 0]
 
 SCRATCH = {
-    "XI": ("sbuf", [128, S], "int32"), "RAW": ("sbuf", [128, 1184], "int32"), "SR": ("sbuf", [128, 56], "int32"),
-    "RT": ("sbuf", [128, O], "int32"), "CW": ("sbuf", [128, S + 8], "int32"),
-    "L16": ("sbuf", [128, 1184], "uint16"), "SR16": ("sbuf", [128, 56], "uint16"), "O16": ("sbuf", [128, 112], "uint16"),
-    "LS16": ("sbuf", [128, 224], "uint16"), "LF": ("sbuf", [128, 224], "float32"),
-    "LO": ("sbuf", [128, 56], "int32"), "HI": ("sbuf", [128, 56], "int32"), "LM": ("sbuf", [128, 56], "int32"),
-    "PI": ("sbuf", [128, 56], "int32"), "PN": ("sbuf", [128, 8], "int32"), "PH": ("sbuf", [128, 8], "int32"),
-    "M": ("sbuf", [128, 8], "float32"), "GT": ("sbuf", [128, 1792], "float32"), "TT": ("sbuf", [128, 1792], "float32"),
-    "Z": ("sbuf", [128, 512], "bfloat16"), "ID": ("sbuf", [128, 384], "bfloat16"), "SEL": ("sbuf", [128, 512], "bfloat16"),
+    "XI": ("sbuf", [128, S], "int32"), "RAW": ("sbuf", [128, 224], "int32"), "RAC": ("sbuf", [128, 6, 160], "int32"),
+    "SR": ("sbuf", [128, 64], "int32"), "RT": ("sbuf", [128, O], "int32"),
+    "CW": ("sbuf", [128, S], "int32"), "CX": ("sbuf", [128, R], "int32"),
+    "L16": ("sbuf", [128, 1184], "uint16"), "SR16": ("sbuf", [128, 64], "uint16"), "O16": ("sbuf", [128, 64], "uint16"),
+    "LS16": ("sbuf", [128, 256], "uint16"), "GT": ("sbuf", [128, 1024], "uint16"),
+    "LO": ("sbuf", [128, 64], "int32"), "LM": ("sbuf", [128, 64], "float32"), "PI": ("sbuf", [128, 64], "float32"),
+    "PZ": ("sbuf", [128, 4, 2, 16], "float32"), "PT": ("sbuf", [128, 4, 2, 16], "float32"), "OF": ("sbuf", [128, 64], "float32"),
+    "PN": ("sbuf", [128, 8], "int32"), "PH": ("sbuf", [128, 8], "int32"), "M": ("sbuf", [128, 8], "float32"),
+    "Z": ("sbuf", [128, 512], "bfloat16"), "CO": ("sbuf", [128, 512], "bfloat16"), "ID": ("sbuf", [128, 384], "bfloat16"),
+    "IDF": ("sbuf", [128, 128], "float32"), "SEL": ("sbuf", [128, 512], "bfloat16"),
     "RB": ("sbuf", [128, O], "bfloat16"), "K": ("sbuf", [128, R], "bfloat16"), "KS": ("sbuf", [128, O], "bfloat16"),
     "X1": ("sbuf", [128, S + O], "bfloat16"), "X2": ("sbuf", [128, S + O], "float32"),
     "HF": ("sbuf", [128, 4 * HW], "bfloat16"), "E": ("sbuf", [128, 2 * (S + O)], "bfloat16"),
     "SB": ("sbuf", [128, 7 * O], "bfloat16"), "XS2": ("sbuf", [128, O], "float32"),
-    "PL": ("sbuf", [128, 6 * S], "bfloat16"), "PS": ("sbuf", [128, 6 * O], "bfloat16"),
+    "PL": ("sbuf", [128, 6 * S], "bfloat16"), "PS": ("sbuf", [128, 6 * O], "bfloat16"), "RUN": ("sbuf", [128, S], "float32"),
     "U": ("sbuf", [128, O + R], "float32"), "PP": ("sbuf", [128, O + R], "float32"), "A1": ("sbuf", [128, O + R], "bfloat16"),
     "YB": ("sbuf", [128, S], "float32"), "ACC": ("psum", [128, 4096], "float32"),
 }
-SEMAPHORES = (["cV", "cS", "cP", "cG", "sent", "stored", "dsp", "drx", "drate", "dreac", "dlist", "dcr", "dcs"]
-              + ["dx%d" % i for i in range(3)] + ["arr%d" % i for i in range(8)])
-XC = [0, 1024, 2048, 2560]
+SEMAPHORES = (["cV", "cS", "cP", "cG", "sent", "stored", "dsr", "drate", "dreac", "dlist", "dcr", "dcs", "dwr", "dws"]
+              + ["dx%d" % i for i in range(2)] + ["arr%d" % i for i in range(8)])
+XC = [0, 1024, 2560]
 
+RUNS = "r0.3 r0.4 r1.3 r1.4 r2.3 r2.4 r3.3 r0.5 r4.3 r1.5 r5.3 r3.4 r2.5 r4.4 r3.5 r5.4 r4.5 r5.5"
 ORDER = {
-    "A": ("u0s u03 u04 p0s u00 u01 u02 p03 p01 p00 p02 p04 h02", "a0s a01 h0s a03 a00 a04 a02 h03 h01 h00 h04"),
-    "B": ("g1s g0s g24 g25 g30 e0s g33 g34 g35 g21 g22 g12 g03 g04 e02 e00 e01 e03 e05 e04",
-          "g2s g3s g00 g01 g02 g15 g20 g31 g32 g05 g10 g11 g13 g23 g14"),
-    "C": ("g0s g11 e0s g10 g03 e01 e00 e02 e03 e04", "g1s g00 g01 g12 g02 g13 g14 g04"),
-    "D": ("g3s g4s g5s g31 g32 g33 e0s g14 g15 g20 g41 g42 g43 g51 g52 g53 g54 g24 g25 g30 e01 e02 e03 e00 e04 e05",
-          "g0s g1s g2s g10 g11 g12 g13 g21 g22 g23 g01 g02 g03 g00 g34 g50 g40 g04 g05 g44 g45 g55 g35"),
-    "Z": ("g20 g21 g30 g31 g41 g42 g05 g10 g11 g02 g03 e00 e01 g43 g14 g15 e03 g54 g55 e02 g24 e05 e04",
-          "g33 g34 g35 g40 g00 g01 g50 g51 g12 g13 g52 g53 g23 g22 g32 g44 g45 g04 g25"),
+    "A": ("u1.f u1.n p.f p.n u1.4 u1.0 u1.1 p.0 u1.23 p.1 p.4 p.2 p.3 h.4", "a0.f a0.n a0.4 h.f h.n a0.0 a0.1 a0.23 h.0 h.1 h.2 h.3"),
+    "B": ("g0.s g1.s g0.3 e.s g1.3 g01.0 g01.1 g01.4 g01.2 g0.5 e.34 e.2 e.5",
+          "g2.s g3.s g23.3 g23.0 g23.1 g23.4 g23.2 g123.5 e.01"),
+    "C": ("g0.f g0.n g0.3 e.f e.n g0.1 g0.4 g0.2 e.0 e.1 e.2 e.3", "g1.f g1.n g0.0 g1.0 g1.1 g1.2 g1.4 g1.3 e.4"),
+    "D": ("g3.s g4.s g5.s r0.3 e.s " + RUNS[5:], "g0.s g1.s g2.s g012345.0 g012345.1 g012345.2 e.01 e.2"),
+    "Z": (RUNS, "g012345.0 g012345.1 e.0 g012.2 g345.2 e.1 e.2"),
 }
-SCHED = {k: [[(u[0], int(u[1]), -1 if u[2] == "s" else int(u[2])) for u in q.split()] for q in v] for k, v in ORDER.items()}
+SEND = {"s": -1, "f": -2, "n": -3}
 
 
-def spans(chunks):
-    out, a = {-1: (0, O)}, 0
+def calls(text):
+    out = []
+    for word in text.split():
+        head, chunks = word.split(".")
+        out.append((head[0], [int(p) for p in head[1:]], [SEND[c] if c in SEND else int(c) for c in chunks], word))
+    return out
+
+
+def spans(chunks, far):
+    out, a = {-1: (0, O), -2: (0, far), -3: (far, O - far)}, 0
     for c, n in enumerate(chunks):
-        out[c] = (a, a + n)
+        out[c] = (a, n)
         a += n
     return out
-
-
-def calls_of(seq, sp):
-    out, top = [], max(sp)
-    for w, p, c in seq:
-        n = sp[c][1] - sp[c][0]
-        if out and out[-1][0] == w and out[-1][2] + n <= 4096:
-            _, us, m = out[-1]
-            p1, c1 = us[-1]
-            if c < 0 or c1 < 0:
-                join = c == c1 and p == p1 + 1
-            elif w in "ep":
-                join = c == c1 + 1 and m == 512 * len(us)
-            else:
-                join = (p, c) == ((p1, c1 + 1) if c1 < top else (p1 + 1, 0))
-            if join:
-                out[-1] = (w, us + [(p, c)], m + n)
-                continue
-        out.append((w, [(p, c)], n))
-    return out
-
-
-def needs(call, planes, direct):
-    w, us, _ = call
-    if w == "e":
-        return [("m", p, c) for p in range(planes) for _, c in us]
-    if w == "p":
-        return [(v, 0, c) for v in "mu" for _, c in us]
-    if w == "q":
-        return [("u", 0, c) for _, c in us]
-    if w == "h":
-        return [("q" if c in direct else "p", 0, c) for _, c in us]
-    return []
-
-
-def plan(seqs, chunks, planes):
-    sp = spans(chunks)
-    direct = set(c for s in seqs for w, _, c in s if w == "q")
-    cl = [calls_of(s, sp) for s in seqs]
-    at, free, done, pe, order = [0, 0], [0.0, 0.0], {}, 0.0, []
-    while at[0] < len(cl[0]) or at[1] < len(cl[1]):
-        best = None
-        for e in (0, 1):
-            if at[e] < len(cl[e]):
-                k = cl[e][at[e]]
-                nd = needs(k, planes, direct)
-                if all(d in done for d in nd):
-                    t = max([free[e]] + [done[d] + 170 for d in nd]) + (55, 70)[e] + k[2] * (1.56 if k[0] in "gauq" else 1.0)
-                    if best is None or t < best[0]:
-                        best = (t, e, k)
-        t, e, k = best
-        free[e] = t
-        at[e] += 1
-        for p, c in k[1]:
-            done[(k[0], p, c)] = t
-            if k[0] in "ga":
-                pe = max(pe, t + 170) + 60 + 0.5 * (sp[c][1] - sp[c][0])
-                done[("m", p, c)] = pe
-                order.append((p, c))
-    return order
 
 
 def shares(core, T, topo):
@@ -145,204 +96,245 @@ def rank_program(g, core, T, topo):
     mine = shares(core, T, topo)
     arrive = sum(len(shares(c, T, topo)[core]) for c in T.cores if c != core)
     sent = sum(len(v) for v in mine.values())
+    away = [m for m in range(N - 1) if topo.chip(T.cores[(rank + 1 + m) % N]) != topo.chip(core)]
+    m0, far = away[0], len(away) * B
 
-    def send(rnd, src, s0, dst, d0, dep):
+    def send(rnd, src, s0, dst, d0, c, dep):
         tr = []
-        for m in range(N - 1):
+        a, n = spans([], far)[c]
+        for b in range(a // B, (a + n) // B):
+            m = (b + m0) % (N - 1)
             d = T.cores[(rank + 1 + m) % N]
             rid, pid, _ = topo.addr(d)
             k = N - 2 - m
             tr.append(RemoteDMATransfer(dst_ids=[DstId(rid=rid, pnc=pid)], dma_engine_mask=sum(1 << e for e in mine[d]),
-                                        remote_sem=T.sem["arr%d" % rnd], src=src[:, s0 + m * B:s0 + (m + 1) * B],
+                                        remote_sem=T.sem["arr%d" % rnd], src=src[:, s0 + b * B:s0 + (b + 1) * B],
                                         dst=dst[:, d0 + k * B:d0 + (k + 1) * B]))
         add("G", None, lambda: g.remote_dma_fused(tr, local_sem=T.sem.sent), [dep], "none")
 
     def vop(name, fn, deps=()):
         add("V", name, fn, deps)
 
-    dma("S", T.SR[:, 0:28], T.spsend[:], "dsp")
-    for i in range(3):
+    pieces = [(0, 4 * m0, 28), (28 - 4 * m0, 0, 4 * m0)][:2 if m0 else 1]
+    for h, lst in enumerate((T.spsend, T.rxsend)):
+        for to, a, b in pieces:
+            dma("SY"[h], T.SR[:, 32 * h + to:32 * h + to + b - a], lst[:, a:b], "dsr")
+    for i in range(2):
         dma("Y", T.XI[:, XC[i]:XC[i + 1]], T.x[:, XC[i]:XC[i + 1]], "dx%d" % i)
-    dma("S", T.SR[:, 28:56], T.rxsend[:], "drx")
     dma("S", T.RT[0:32, :], T.rate[:], "drate")
+    dma("Y", T.RAW[:], T.reac[:], "dreac")
     for c in range(2):
-        dma("Y", T.CW[6 + c:128:16, 8:8 + R], T.reac[:, c * 112:(c + 1) * 112], "dcr", ["cw0"])
-    dma("Y", T.RAW[:, 0:224], T.reac[:], "dreac")
+        dma("Y", T.CX[c:128:16, :], T.reac[:, c * 112:(c + 1) * 112], "dcr", ["cx0"])
     for c in range(6):
         src = T.cons[:, c * 160:(c + 1) * 160] if c < 4 else T.prod[:, (c - 4) * 160:(c - 3) * 160]
-        dma("Y", T.CW[c:128:16, 8:8 + S], src, "dcs")
-    dma("Y", T.RAW[:, 224:864], T.cons[:], "dlist")
-    dma("Y", T.RAW[:, 864:1184], T.prod[:], "dlist")
+        dma("Y", T.CW[c:128:16, :], src, "dcs", ["cw0"])
+    dma("Y", T.RAC[:, 0:4, :], T.cons[:], "dlist")
+    dma("Y", T.RAC[:, 4:6, :], T.prod[:], "dlist")
 
     vop("z", lambda: V.memset(T.Z[:], 0.0))
+    vop("pad", lambda: V.memset(T.SR[:, 28:32], 0))
+    vop("pad", lambda: V.memset(T.SR[:, 60:64], 0))
     vop("cw0", lambda: V.memset(T.CW[:], 0))
-    vop("none", lambda: V.memset(T.HF[:, R + O:4 * HW:HW], OFF))
     add("G", "pn", lambda: g.iota(T.PN[:, 0:1], [[0, 1]], 0, 1))
+    add("G", "cx0", lambda: g.iota(T.CX[:], [[0, R]], 0, 0))
     add("G", "sel", lambda: g.affine_select(T.SEL[0:32, :], T.Z[0:32, :], [[-1, 4], [-4, 8], [0, 16]], A.not_equal, 1.0, 0, 1), ["z"])
-    for i, v in enumerate((1.0, -1.0, -16384.0)):
+    for i, v in enumerate((1.0, -1.0, -BIG)):
         add("G", "id%d" % i, lambda i=i, v=v: g.affine_select(T.ID[:, i * 128:(i + 1) * 128], T.Z[:, 0:128], [[-1, 128]], A.not_equal, v, 0, 1), ["z"])
-    PLUS, MINUS, BIG = T.ID[:, 0:128], T.ID[:, 128:256], T.ID[:, 256:384]
+    PLUS, MINUS, VETO = T.ID[:, 0:128], T.ID[:, 128:256], T.ID[:, 256:384]
+
     vop("ph", lambda: V.tensor_scalar(T.PH[:, 0:1], T.PN[:, 0:1], 4, 1, A.arith_shift_right, A.bitwise_and), ["pn"])
-    vop("sr16", lambda: V.tensor_copy(T.SR16[:], T.SR[:]), [("dsp", 16), ("drx", 16)])
-    vop("lo", lambda: V.tensor_scalar(T.LO[:], T.SR[:], 15, None, A.bitwise_and))
-    vop("hi", lambda: V.tensor_scalar(T.HI[:], T.SR[:], 4, None, A.arith_shift_right))
-    vop("m1", lambda: V.tensor_copy(T.M[:, 1:2], T.PH[:, 0:1]), ["ph"])
-    vop("m0", lambda: V.tensor_scalar(T.M[:, 0:1], T.PH[:, 0:1], -1.0, 1.0, A.mult, A.add))
-    vop("lm0", lambda: V.tensor_scalar(T.LM[:, 0:28], T.LO[:, 0:28], 160.0, 8.0, A.mult, A.add), ["lo"])
-    vop("lm1", lambda: V.tensor_scalar(T.LM[:, 28:56], T.LO[:, 28:56], 112.0, 8.0, A.mult, A.add))
+    vop("lo", lambda: V.tensor_scalar(T.LO[:], T.SR[:], 15, None, A.bitwise_and), [("dsr", 32 * len(pieces)), "pad"])
+    vop("m1", lambda: V.tensor_scalar(T.M[:, 1:2], T.PH[:, 0:1], 1.0 / 16, None, A.mult), ["ph"])
+    vop("m0", lambda: V.tensor_scalar(T.M[:, 0:1], T.PH[:, 0:1], -1.0 / 16, 1.0 / 16, A.mult, A.add))
+    for h, width in enumerate((160, 112)):
+        vop("lm", lambda h=h, width=width: V.tensor_scalar(T.LM[:, 32 * h:32 * h + 32], T.LO[:, 32 * h:32 * h + 32], 16.0 * width - 1, None, A.mult), ["lo"])
+    vop("sr16", lambda: V.tensor_copy(T.SR16[:], T.SR[:]))
+    vop("pi", lambda: V.tensor_tensor(T.PI[:], T.LM[:], T.SR[:], A.add), ["lm"])
     vop("rb", lambda: V.tensor_copy(T.RB[0:32, :], T.RT[0:32, :]), [("drate", 16)])
-    vop("pi", lambda: V.tensor_tensor(T.PI[:], T.LM[:], T.HI[:], A.add), ["lm1", "hi"])
-    vop("x0", lambda: V.tensor_copy(T.X1[:, XC[0]:XC[1]], T.XI[:, XC[0]:XC[1]]), [("dx0", 16)])
     for h in range(2):
-        vop("o%d" % h, lambda h=h: V.tensor_scalar(T.O16[:, h:112:2], T.PI[:], T.M[:, h:h + 1], None, A.mult), ["pi", "m0", "m1"])
-    vop("x1", lambda: V.tensor_copy(T.X1[:, XC[1]:XC[2]], T.XI[:, XC[1]:XC[2]]), [("dx1", 16)])
-    vop("xs", lambda: V.tensor_copy(T.SB[:, 0:O], T.XI[:, 0:S].indirect(T.SR16[:, 0:28])), [("dx2", 16), "sr16"])
-    send(0, T.SB, 0, T.X1, S, "xs")
-    vop("x2", lambda: V.tensor_copy(T.X1[:, XC[2]:XC[3]], T.XI[:, XC[2]:XC[3]]))
+        vop("pz", lambda h=h: V.tensor_scalar(T.PZ[:, :, h, :], T.PI[:], T.M[:, h:h + 1], None, A.mult), ["pi", "m0", "m1"])
+    vop("none", lambda: V.memset(T.HF[:, R + O:2 * HW:HW], OFF))
+    vop("none", lambda: V.memset(T.HF[:, 2 * HW + R + O:4 * HW:HW], 0.0))
+    vop("pt", lambda: V.transpose(T.PT[:], T.PZ[:]), ["pz"])
+    for h in range(2):
+        vop("of", lambda h=h: V.tensor_tensor(T.OF[:, h:64:2], T.PT[:, h:4:2, 0, :], T.PT[:, h:4:2, 1, :], A.add), ["pt"])
+    vop("x0", lambda: V.tensor_copy(T.X1[:, XC[0]:XC[1]], T.XI[:, XC[0]:XC[1]]), [("dx0", 16)])
+    vop("o16", lambda: V.tensor_copy(T.O16[:], T.OF[:]), ["of"])
+    for c in (-2, -3):
+        a, n = spans([], far)[c]
+        vop("xs%d" % c, lambda a=a, n=n: V.tensor_copy(T.SB[:, a:a + n], T.XI[:, 0:S].indirect(T.SR16[:, a // 16:(a + n) // 16])), [("dx1", 16), "sr16"])
+        send(0, T.SB, 0, T.X1, S, c, "xs%d" % c)
+    vop("gr", lambda: V.tensor_copy(T.GT[:, 512:1024], T.CX[:, 0:R].indirect(T.O16[:, 32:64])), [("dcr", 32), "o16"])
+    for c in range(2):
+        dma("S", T.LS16[:, (6 + c) * 32:(7 + c) * 32], T.GT[c:128:16, 512:1024], "dwr", ["gr"])
+    vop("x1", lambda: V.tensor_copy(T.X1[:, XC[1]:XC[2]], T.XI[:, XC[1]:XC[2]]))
+    vop("lr", lambda: V.tensor_copy(T.L16[:, 0:224], T.RAW[:]), [("dreac", 16)])
+    vop("gs", lambda: V.tensor_copy(T.GT[:, 0:512], T.CW[:, 0:S].indirect(T.O16[:, 0:32])), [("dcs", 96)])
+    for c in range(6):
+        dma("Y", T.LS16[:, c * 32:(c + 1) * 32], T.GT[c:128:16, 0:512], "dws", ["gs"])
+    for c in range(len(CS)):
+        a, n = spans(CS, far)[c]
+        add("G", "ll", lambda a=a // 16, n=n // 16: g.affine_select(T.L16[:, 224 + 6 * a:224 + 6 * (a + n)], T.RAC[:, :, a:a + n],
+                                                                    [[0, 6 * n]], A.is_equal, 0.0, 0, 0), [("dlist", 32)])
 
     for r in range(4):
         add("P", "km%d" % r, lambda r=r: P.matmul(T.ACC[:, r * 512:r * 512 + O], T.SEL[0:32, r * 128:(r + 1) * 128], T.RB[0:32, :], True, True), ["sel", "rb"])
+    ks = len(ops["S"]) - 2
     for r in range(4):
         add("S", "k%d" % r, lambda r=r: Sc.activation(T.K[:, r * O:(r + 1) * O], T.ACC[:, r * 512:r * 512 + O], F.Identity, scale=1.0 / 1024), ["km%d" % r])
-    add("S", "ks", lambda: Sc.activation(T.KS[:], T.K[:, 0:R].indirect(T.SR16[:, 28:56]), F.Identity), ["k3", "sr16"])
-
-    def compose(tag, half, sem, part):
-        a, b = half * 896, (half + 1) * 896
-        cs = range(0, 6) if half == 0 else range(6, 8)
-        if part == 0:
-            vop(tag + "g", lambda: V.tensor_copy(T.GT[:, a:b], T.CW[:, 0:S + 8].indirect(T.O16[:, half * 56:(half + 1) * 56])), ["o0", "o1"] + sem)
-        elif part == 1:
-            vop(tag + "t", lambda: V.transpose(T.TT[:, a:b], T.GT[:, a:b]), [tag + "g"])
-        elif part == 2:
-            for c in cs:
-                vop(tag + "a%d" % c, lambda c=c: V.tensor_tensor(T.LF[:, c * 28:(c + 1) * 28], T.TT[:, a + c:b:32], T.TT[:, a + 16 + c:b:32], A.add), [tag + "t"])
-        else:
-            vop(tag, lambda: V.tensor_copy(T.LS16[:, cs[0] * 28:(cs[-1] + 1) * 28], T.LF[:, cs[0] * 28:(cs[-1] + 1) * 28]), [tag + "a%d" % cs[-1]])
-
-    vop("lr", lambda: V.tensor_copy(T.L16[:, 0:224], T.RAW[:, 0:224]), [("dreac", 16)])
-    for part in range(4):
-        compose("cr", 1, [("dcr", 32), ("dcs", 96)], part)
-        compose("cs", 0, [], part)
+    add("S", "ks", lambda: Sc.activation(T.KS[:], T.K[:, 0:R].indirect(T.SR16[:, 32:60]), F.Identity), ["k3", "sr16"])
+    add("S", "co", lambda: Sc.activation(T.CO[:], T.Z[:], F.Identity, bias=OFF), ["z"])
+    add("S", "idf", lambda: Sc.activation(T.IDF[:], PLUS, F.Identity), ["id0"])
+    ops["S"][ks:] = ops["S"][ks + 2:] + ops["S"][ks:ks + 2]
 
     def last(e):
-        return [o[0] for o in ops[e] if o[0] is not None][-1]
-
-    def bank(c, n):
-        return T.ACC[:, (c + 1) * 512:(c + 1) * 512 + n]
+        return [o[0] for o in ops[e] if o[3] is None][-1]
 
     def phase(kind, step, key):
         ph = "%s%d" % (kind, step)
         rnd = 4 * step + "ABCD".index(kind)
-        chunks = CR if kind in "AC" else CS
-        W = R if kind in "AC" else S
+        rx = kind in "AC"
+        sp = spans(CR if rx else CS, far)
         planes = {"A": 1, "B": 4, "C": 2, "D": 6}[kind]
-        sp = spans(chunks)
-        seqs = SCHED[key]
-        direct = set(c for s in seqs for w, _, c in s if w == "q")
         X = T.X1 if step == 0 else T.X2
-        XS = T.SB[:, 0:O] if step == 0 else T.XS2[:]
+        XS = T.SB if step == 0 else T.XS2
         h0, f0, e0 = step * HW, (2 + step) * HW, step * (S + O)
         hs, es, fs = (1 + 3 * step) * O, (2 + 3 * step) * O, (3 + 3 * step) * O
         win = {"A": X[:, 0:S + O], "B": T.HF[:, h0:h0 + R + O + 1], "C": T.E[:, e0:e0 + S + O], "D": T.HF[:, f0:f0 + R + O + 1]}[kind]
-        gate = [last("V"), last("S"), ("arr%d" % rnd, arrive)]
-        maker, sign, stores = {}, {}, []
+        gate = [last("V"), last("S"), ("arr%d" % rnd, arrive)] + {0: [("dwr", 32)], 1: [("dws", 96), "ll"]}.get(rnd, [])
+        cl = {e: calls(t) for e, t in zip("VS", ORDER[key])}
+        maker, stores = {}, []
+
+        def place(p, c):
+            a, n = sp[c]
+            return p * O + a if c < 0 else p * R + a if rx else 6 * a + p * n
 
         def src(p, c, n):
-            if c < 0:
-                b = (168 if kind in "AC" else 0) + p * 28
-                return win.indirect(T.LS16[:, b:b + n // 16])
-            b = (0 if kind in "AC" else 224) + (p * W + sp[c][0]) // 16
-            return win.indirect(T.L16[:, b:b + n // 16])
+            b = 32 * (p + (6 if rx else 0)) + sp[c][0] // 16 if c < 0 else place(p, c) // 16 + (0 if rx else 224)
+            return win.indirect((T.LS16 if c < 0 else T.L16)[:, b:b + n // 16])
 
         def plane(p, c, n):
-            return T.PS[:, p * O:p * O + n] if c < 0 else T.PL[:, p * W + sp[c][0]:p * W + sp[c][0] + n]
+            return (T.PS if c < 0 else T.PL)[:, place(p, c):place(p, c) + n]
+
+        def bank(c, n):
+            b = (BANKS_A[c] if kind == "A" else c + 1) if c >= 0 else 7 if c == -3 else 0
+            return T.ACC[:, b * 512:b * 512 + n]
+
+        def own(buf, base, sbuf, s0, c, n):
+            a = sp[c][0] + (s0 if c < 0 else base)
+            return (sbuf if c < 0 else buf)[:, a:a + n]
 
         def col(buf, c, n):
-            return buf[:, 0:O] if c < 0 else buf[:, O + sp[c][0]:O + sp[c][0] + n]
+            return own(buf, O, buf, 0, c, n)
 
-        def own(buf, base, sbuf, c, n):
-            return sbuf if c < 0 else buf[:, base + sp[c][0]:base + sp[c][0] + n]
-
-        def make(e, w, p, c, n):
+        def make(e, w, ps, cs):
+            c, n = cs[0], sum(sp[k][1] for k in cs)
             if w == "g":
-                o, i = plane(p, c, n), src(p, c, n)
-                if e == "V":
-                    if kind == "B":
+                o, i = plane(ps[0], c, n * len(ps)), src(ps[0], c, n * len(ps))
+                if kind == "B":
+                    if e == "V":
                         return lambda: V.tensor_scalar(o, i, OFF + 3, OFF + 3, A.min, A.subtract)
-                    return lambda: V.tensor_scalar(o, i, 12.0 if kind == "C" else OFF, None, A.is_lt if kind == "C" else A.subtract)
-                if kind == "D":
-                    return lambda: Sc.activation(o, i, F.Identity, bias=-OFF)
-                return lambda: Sc.activation(o, i, F.Relu, bias=OFF + 3 if kind == "B" else 12.0, scale=-1.0)
+                    return lambda: Sc.activation(o, i, F.Relu, bias=OFF + 3, scale=-1.0)
+                if kind == "C":
+                    if e == "V":
+                        return lambda: V.tensor_scalar(o, i, 12.0, OFF / BIG, A.is_lt, A.add)
+                    return lambda: Sc.activation(o, i, F.Relu, bias=12.0, scale=-1.0)
+                return (lambda: V.tensor_copy(o, i)) if e == "V" else (lambda: Sc.activation(o, i, F.Identity))
+            new = T.X2 if step == 0 else T.YB
+            if w == "r":
+                p, run = ps[0], own(T.RUN, 0, None, 0, c, n)
+                o, i = own(new, 0, None, 0, c, n) if p == 5 else run, own(X, 0, None, 0, c, n) if p == 0 else run
+                return lambda: V.tensor_tensor(o, src(p, c, n), i, A.subtract if p in (0, 4) else A.add)
             if w == "e":
                 if kind == "C":
-                    o = own(T.HF, f0, T.SB[:, fs:fs + O], c, n)
-                    return lambda: V.tensor_scalar(o, bank(c, n), OFF, OFF + 3, A.max, A.min)
-                if kind == "B":
-                    o = own(T.E, e0, T.SB[:, es:es + O], c, n)
-                else:
-                    o = own(T.X2 if step == 0 else T.YB, 0, T.XS2[:], c, n)
-                return lambda: V.tensor_tensor(o, bank(c, n), own(X, 0, XS, c, n), A.add)
+                    o = own(T.HF, f0, T.SB, fs, c, n)
+                    if e == "V":
+                        return lambda: V.tensor_scalar(o, bank(c, n), 0.0, 3.0, A.max, A.min)
+                    return lambda: Sc.activation(o, bank(c, n), F.Relu)
+                o = own(T.E, e0, T.SB, es, c, n) if kind == "B" else own(new, 0, T.XS2, 0, c, n)
+                if e == "V":
+                    return lambda: V.tensor_tensor(o, bank(c, n), own(X, 0, XS, 0, c, n), A.add)
+                return lambda: Sc.activation(o, bank(c, n), F.Identity)
             if w == "u":
-                return lambda: V.tensor_tensor(col(T.U, c, n), src(1, c, n), own(T.K, 0, T.KS[:], c, n), A.mult)
-            if w == "q":
-                return lambda: V.tensor_tensor(col(T.PP, c, n), src(0, c, n), col(T.U, c, n), A.mult)
-            if w == "p":
-                return lambda: V.tensor_tensor(col(T.PP, c, n), bank(c, n), col(T.U, c, n), A.mult)
+                return lambda: V.tensor_tensor(col(T.U, c, n), src(1, c, n), own(T.K, 0, T.KS, 0, c, n), A.mult)
+            if w in "pq":
+                return lambda: V.tensor_tensor(col(T.PP, c, n), bank(c, n) if w == "p" else src(0, c, n), col(T.U, c, n), A.mult)
             if w == "a":
                 return lambda: Sc.activation(col(T.A1, c, n), src(0, c, n), F.Identity)
-            o = own(T.HF, h0, T.SB[:, hs:hs + O], c, n)
+            o = own(T.HF, h0, T.SB, hs, c, n)
             shift = OFF - 1023.0 / 2048
             if e == "V":
-                return lambda: V.tensor_scalar(o, col(T.PP, c, n), shift, None, A.add)
+                return lambda: V.tensor_scalar(o, col(T.PP, c, n), 3.5, shift, A.min, A.add)
             return lambda: Sc.activation(o, col(T.PP, c, n), F.Identity, bias=shift)
 
-        cl = {"V": calls_of(seqs[0], sp), "S": calls_of(seqs[1], sp)}
+        due, by, reader = [], {}, {}
         for e in "VS":
-            for w, us, n in cl[e]:
-                for p, c in us:
-                    maker[(w, p, c)] = "%s%s%d_%d" % (ph, w, us[0][0], us[0][1])
-                    if w == "g":
-                        sign[(p, c)] = e
-                if w == "e":
-                    stores.append((maker[(w,) + us[0]], sp[us[0][1]][0], n))
-        seen = {}
-        if kind == "C":
-            for c in [-1] + list(range(len(chunks))):
-                n = sp[c][1] - sp[c][0]
-                add("P", "%sf%d" % (ph, c), lambda c=c, n=n: P.matmul(bank(c, n), PLUS, own(T.HF, h0, T.SB[:, hs:hs + O], c, n), True, False), gate[:2])
-        for p, c in plan(seqs, chunks, planes):
-            n = sp[c][1] - sp[c][0]
-            seen[c] = seen.get(c, 0) + 1
+            t = 0
+            for w, ps, cs, word in cl[e]:
+                t += 60 + sum(sp[c][1] for c in cs) * (1.5 * len(ps) if ps else 1)
+                for c in cs:
+                    for p in ps or [0]:
+                        maker[("p" if w == "q" else w, p, c)] = ph + word
+                        if w in "ga":
+                            due.append((t, p, c))
+                            by[(p, c)] = e
+                    if w == "e":
+                        reader[c] = e
+                if w == "e" or (w, ps) == ("r", [5]):
+                    stores.append((t, e, ph + word, sp[cs[0]][0], sum(sp[c][1] for c in cs)))
+        terms = {}
+        due.sort()
+        if kind == "D":
+            at = len([d for d in due if d[2] < 0])
+            due[at:at] = [(0, None, c) for c in sorted(reader) if c >= 0]
+        for _, p, c in due:
+            n = sp[c][1]
+            if c not in terms:
+                terms[c] = []
+                if kind == "C":
+                    terms[c].append((PLUS, own(T.HF, h0, T.SB, hs, c, n)))
+                    if by[(0, c)] == "S":
+                        terms[c].append((MINUS, T.CO[:, 0:n]))
+                elif reader.get(c) == "S" and kind != "B":
+                    terms[c].append((PLUS if step == 0 else T.IDF[:], own(X, 0, None, 0, c, n)))
+                for i, (lhs, rhs) in enumerate(terms[c]):
+                    add("P", "%st%d_%d" % (ph, i, c), lambda c=c, n=n, lhs=lhs, rhs=rhs, i=i: P.matmul(bank(c, n), lhs, rhs, i == 0, False), gate[:2] + ["id2"])
+            if p is None:
+                continue
             if kind == "A":
                 lhs, rhs, dep = PLUS, col(T.A1, c, n), maker[("a", p, c)]
             else:
                 rhs, dep = plane(p, c, n), maker[("g", p, c)]
-                lhs = BIG if kind == "C" else (MINUS if (sign[(p, c)] == "V" if kind == "B" else p < 4) else PLUS)
+                lhs = VETO if kind == "C" else MINUS if (by[(p, c)] == "V" if kind == "B" else p < 4) else PLUS
+            first = not terms[c] and (kind, reader.get(c)) != ("B", "S")
+            terms[c].append(p)
             maker[("m", p, c)] = "%sm%d_%d" % (ph, p, c)
-            add("P", maker[("m", p, c)], lambda c=c, n=n, lhs=lhs, rhs=rhs, a=(seen[c] == 1 and kind != "C"), z=(seen[c] == planes):
-                P.matmul(bank(c, n), lhs, rhs, a, z), [dep, "id2"])
+            free = [maker[("p", 0, -2)]] if kind == "A" and c >= 0 and BANKS_A[c] == 0 else []
+            add("P", maker[("m", p, c)], lambda c=c, n=n, lhs=lhs, rhs=rhs, a=first, z=sum(isinstance(v, int) for v in terms[c]) == planes:
+                P.matmul(bank(c, n), lhs, rhs, a, z), [dep, "id2"] + free)
+            if (kind, c) == ("A", -3):
+                for k in range(2):
+                    add("P", "%sx%d" % (ph, k), lambda k=k: P.matmul(T.ACC[:, (k + 1) * 512:(k + 2) * 512], PLUS if step == 0 else T.IDF[:],
+                                                                      X[:, k * 512:(k + 1) * 512], True, False))
         for e in "VS":
-            for k in cl[e]:
-                add(e, maker[(k[0],) + k[1][0]], make(e, k[0], k[1][0][0], k[1][0][1], k[2]), gate + [maker[d] for d in needs(k, planes, direct)])
-        out = maker.get(("h" if kind == "A" else "e", 0, -1))
-        if out is not None:
-            if kind == "D":
-                send(rnd + 1, T.XS2, 0, T.X2, S, out)
-            elif kind == "B":
-                send(rnd + 1, T.SB, es, T.E, e0 + S, out)
-            else:
-                send(rnd + 1, T.SB, hs if kind == "A" else fs, T.HF, (h0 if kind == "A" else f0) + R, out)
+            for w, ps, cs, word in cl[e]:
+                need = {"e": [("m", p) for p in range(planes)], "p": [("m", 0), ("u", 1)], "q": [("u", 1)], "h": [("p", 0)],
+                        "r": [("r", p - 1) for p in ps if p]}.get(w, [])
+                add(e, ph + word, make(e, w, ps, cs), gate + [maker[d + (c,)] for d in need for c in cs])
+        for c in SEND.values():
+            out = maker.get(("h" if kind == "A" else "e", 0, c))
+            if out is not None:
+                src_, s0, dst, d0 = {"A": (T.SB, hs, T.HF, h0 + R), "B": (T.SB, es, T.E, e0 + S), "C": (T.SB, fs, T.HF, f0 + R), "D": (T.XS2, 0, T.X2, S)}[kind]
+                send(rnd + 1, src_, s0, dst, d0, c, out)
         return stores
 
     for step in range(2):
         phase("A", step, "A")
-        if step == 0:
-            vop("ll", lambda: V.tensor_copy(T.L16[:, 224:1184], T.RAW[:, 224:1184]), [("dlist", 32)])
         phase("B", step, "B")
         phase("C", step, "C")
         stores = phase("D", step, "D" if step == 0 else "Z")
-    for name, a, n in stores:
-        dma("Y", T.y[:, a:a + n], T.YB[:, a:a + n], "stored", [name])
+    for i, (_, e, name, a, n) in enumerate(sorted(stores)):
+        dma("S" if name == last("S") else "Y", T.y[:, a:a + n], T.YB[:, a:a + n], "stored", [name])
 
     total = {}
     for e in "VSPG":

from concourse.bass import DstId, RemoteDMATransfer
from concourse.mybir import AluOpType, ActivationFunctionType

S, R, B, O = 2560, 1792, 64, 448
OFF = 130.0
BIG = 16384.0
HW = 2256
CS = [512, 512, 256, 512, 512, 256]
CR = [512, 512, 384, 128, 256]
BANKS_A = [3, 4, 5, 6, 0]

SCRATCH = {
    "XI": ("sbuf", [128, S], "int32"), "RAW": ("sbuf", [128, 224], "int32"), "RAC": ("sbuf", [128, 6, 160], "int32"),
    "SR": ("sbuf", [128, 64], "int32"), "RT": ("sbuf", [128, O], "int32"),
    "CW": ("sbuf", [128, S], "int32"), "CX": ("sbuf", [128, R], "int32"),
    "L16": ("sbuf", [128, 1184], "uint16"), "SR16": ("sbuf", [128, 64], "uint16"), "O16": ("sbuf", [128, 64], "uint16"),
    "LS16": ("sbuf", [128, 256], "uint16"), "GT": ("sbuf", [128, 1024], "uint16"),
    "LO": ("sbuf", [128, 64], "int32"), "LM": ("sbuf", [128, 64], "float32"), "PI": ("sbuf", [128, 64], "float32"),
    "PZ": ("sbuf", [128, 4, 2, 16], "float32"), "PT": ("sbuf", [128, 4, 2, 16], "float32"), "OF": ("sbuf", [128, 64], "float32"),
    "PN": ("sbuf", [128, 8], "int32"), "PH": ("sbuf", [128, 8], "int32"), "M": ("sbuf", [128, 8], "float32"),
    "Z": ("sbuf", [128, 512], "bfloat16"), "CO": ("sbuf", [128, 512], "bfloat16"), "ID": ("sbuf", [128, 384], "bfloat16"),
    "IDF": ("sbuf", [128, 128], "float32"), "SEL": ("sbuf", [128, 512], "bfloat16"),
    "RB": ("sbuf", [128, O], "bfloat16"), "K": ("sbuf", [128, R], "bfloat16"), "KS": ("sbuf", [128, O], "bfloat16"),
    "X1": ("sbuf", [128, S + O], "bfloat16"), "X2": ("sbuf", [128, S + O], "float32"),
    "HF": ("sbuf", [128, 4 * HW], "bfloat16"), "E": ("sbuf", [128, 2 * (S + O)], "bfloat16"),
    "SB": ("sbuf", [128, 7 * O], "bfloat16"), "XS2": ("sbuf", [128, O], "float32"),
    "PL": ("sbuf", [128, 6 * S], "bfloat16"), "PS": ("sbuf", [128, 6 * O], "bfloat16"), "RUN": ("sbuf", [128, S], "float32"),
    "U": ("sbuf", [128, O + R], "float32"), "PP": ("sbuf", [128, O + R], "float32"), "A1": ("sbuf", [128, O + R], "bfloat16"),
    "YB": ("sbuf", [128, S], "float32"), "ACC": ("psum", [128, 4096], "float32"),
}
SEMAPHORES = (["cV", "cS", "cP", "cG", "sent", "stored", "dsr", "drate", "dreac", "dlist", "dcr", "dcs", "dwr", "dws"]
              + ["dx%d" % i for i in range(2)] + ["arr%d" % i for i in range(8)])
XC = [0, 1024, 2560]

RUNS = "r0.3 r0.4 r1.3 r1.4 r2.3 r2.4 r3.3 r0.5 r4.3 r1.5 r5.3 r3.4 r2.5 r4.4 r3.5 r5.4 r4.5 r5.5"
ORDER = {
    "A": ("u1.f u1.n p.f p.n u1.4 u1.0 u1.1 p.0 u1.23 p.1 p.4 p.2 p.3 h.4", "a0.f a0.n a0.4 h.f h.n a0.0 a0.1 a0.23 h.0 h.1 h.2 h.3"),
    "B": ("g0.s g1.s g0.3 e.s g1.3 g01.0 g01.1 g01.4 g01.2 g0.5 e.34 e.2 e.5",
          "g2.s g3.s g23.3 g23.0 g23.1 g23.4 g23.2 g123.5 e.01"),
    "C": ("g0.f g0.n g0.3 e.f e.n g0.1 g0.4 g0.2 e.0 e.1 e.2 e.3", "g1.f g1.n g0.0 g1.0 g1.1 g1.2 g1.4 g1.3 e.4"),
    "D": ("g3.s g4.s g5.s r0.3 e.s " + RUNS[5:], "g0.s g1.s g2.s g012345.0 g012345.1 g012345.2 e.01 e.2"),
    "Z": (RUNS, "g012345.0 g012345.1 e.0 g012.2 g345.2 e.1 e.2"),
}
SEND = {"s": -1, "f": -2, "n": -3}


def calls(text):
    out = []
    for word in text.split():
        head, chunks = word.split(".")
        out.append((head[0], [int(p) for p in head[1:]], [SEND[c] if c in SEND else int(c) for c in chunks], word))
    return out


def spans(chunks, far):
    out, a = {-1: (0, O), -2: (0, far), -3: (far, O - far)}, 0
    for c, n in enumerate(chunks):
        out[c] = (a, n)
        a += n
    return out


def shares(core, T, topo):
    far = [c for c in T.cores if topo.chip(c) != topo.chip(core)]
    near = [c for c in T.cores if c != core and c not in far]
    used = topo.engines(core, far[0])
    out = {}
    for group, pool in ((far, used), (near, [e for e in topo.engines(core, near[0]) if e not in used])):
        left = list(pool)
        for i, d in enumerate(group):
            n = 1
            while 2 * n + (len(group) - i - 1) * (len(pool) // len(group)) <= len(left):
                n *= 2
            out[d] = left[:n]
            left = left[n:]
    return out


def rank_program(g, core, T, topo):
    rank = T.rank_of(core)
    if rank is None:
        return
    A, F = AluOpType, ActivationFunctionType
    N = len(T.cores)
    V, Sc, P, Y = g.vector, g.scalar, g.tensor, g.sync
    queue = {"V": V, "S": Sc, "P": P, "G": g, "Y": Y}
    ops = {e: [] for e in queue}
    where = {}

    def add(e, name, fn, deps=(), sem=None):
        ops[e].append((name, fn, list(deps), sem))

    def dma(e, out, in_, sem, deps=()):
        add(e, None, lambda: queue[e].dma_start(out, in_), deps, sem)

    mine = shares(core, T, topo)
    arrive = sum(len(shares(c, T, topo)[core]) for c in T.cores if c != core)
    sent = sum(len(v) for v in mine.values())
    away = [m for m in range(N - 1) if topo.chip(T.cores[(rank + 1 + m) % N]) != topo.chip(core)]
    m0, far = away[0], len(away) * B

    def send(rnd, src, s0, dst, d0, c, dep):
        tr = []
        a, n = spans([], far)[c]
        for b in range(a // B, (a + n) // B):
            m = (b + m0) % (N - 1)
            d = T.cores[(rank + 1 + m) % N]
            rid, pid, _ = topo.addr(d)
            k = N - 2 - m
            tr.append(RemoteDMATransfer(dst_ids=[DstId(rid=rid, pnc=pid)], dma_engine_mask=sum(1 << e for e in mine[d]),
                                        remote_sem=T.sem["arr%d" % rnd], src=src[:, s0 + b * B:s0 + (b + 1) * B],
                                        dst=dst[:, d0 + k * B:d0 + (k + 1) * B]))
        add("G", None, lambda: g.remote_dma_fused(tr, local_sem=T.sem.sent), [dep], "none")

    def vop(name, fn, deps=()):
        add("V", name, fn, deps)

    pieces = [(0, 4 * m0, 28), (28 - 4 * m0, 0, 4 * m0)][:2 if m0 else 1]
    for h, lst in enumerate((T.spsend, T.rxsend)):
        for to, a, b in pieces:
            dma("SY"[h], T.SR[:, 32 * h + to:32 * h + to + b - a], lst[:, a:b], "dsr")
    for i in range(2):
        dma("Y", T.XI[:, XC[i]:XC[i + 1]], T.x[:, XC[i]:XC[i + 1]], "dx%d" % i)
    dma("S", T.RT[0:32, :], T.rate[:], "drate")
    dma("Y", T.RAW[:], T.reac[:], "dreac")
    for c in range(2):
        dma("Y", T.CX[c:128:16, :], T.reac[:, c * 112:(c + 1) * 112], "dcr", ["cx0"])
    for c in range(6):
        src = T.cons[:, c * 160:(c + 1) * 160] if c < 4 else T.prod[:, (c - 4) * 160:(c - 3) * 160]
        dma("Y", T.CW[c:128:16, :], src, "dcs", ["cw0"])
    dma("Y", T.RAC[:, 0:4, :], T.cons[:], "dlist")
    dma("Y", T.RAC[:, 4:6, :], T.prod[:], "dlist")

    vop("z", lambda: V.memset(T.Z[:], 0.0))
    vop("pad", lambda: V.memset(T.SR[:, 28:32], 0))
    vop("pad", lambda: V.memset(T.SR[:, 60:64], 0))
    vop("cw0", lambda: V.memset(T.CW[:], 0))
    add("G", "pn", lambda: g.iota(T.PN[:, 0:1], [[0, 1]], 0, 1))
    add("G", "cx0", lambda: g.iota(T.CX[:], [[0, R]], 0, 0))
    add("G", "sel", lambda: g.affine_select(T.SEL[0:32, :], T.Z[0:32, :], [[-1, 4], [-4, 8], [0, 16]], A.not_equal, 1.0, 0, 1), ["z"])
    for i, v in enumerate((1.0, -1.0, -BIG)):
        add("G", "id%d" % i, lambda i=i, v=v: g.affine_select(T.ID[:, i * 128:(i + 1) * 128], T.Z[:, 0:128], [[-1, 128]], A.not_equal, v, 0, 1), ["z"])
    PLUS, MINUS, VETO = T.ID[:, 0:128], T.ID[:, 128:256], T.ID[:, 256:384]

    vop("ph", lambda: V.tensor_scalar(T.PH[:, 0:1], T.PN[:, 0:1], 4, 1, A.arith_shift_right, A.bitwise_and), ["pn"])
    vop("lo", lambda: V.tensor_scalar(T.LO[:], T.SR[:], 15, None, A.bitwise_and), [("dsr", 32 * len(pieces)), "pad"])
    vop("m1", lambda: V.tensor_scalar(T.M[:, 1:2], T.PH[:, 0:1], 1.0 / 16, None, A.mult), ["ph"])
    vop("m0", lambda: V.tensor_scalar(T.M[:, 0:1], T.PH[:, 0:1], -1.0 / 16, 1.0 / 16, A.mult, A.add))
    for h, width in enumerate((160, 112)):
        vop("lm", lambda h=h, width=width: V.tensor_scalar(T.LM[:, 32 * h:32 * h + 32], T.LO[:, 32 * h:32 * h + 32], 16.0 * width - 1, None, A.mult), ["lo"])
    vop("sr16", lambda: V.tensor_copy(T.SR16[:], T.SR[:]))
    vop("pi", lambda: V.tensor_tensor(T.PI[:], T.LM[:], T.SR[:], A.add), ["lm"])
    vop("rb", lambda: V.tensor_copy(T.RB[0:32, :], T.RT[0:32, :]), [("drate", 16)])
    for h in range(2):
        vop("pz", lambda h=h: V.tensor_scalar(T.PZ[:, :, h, :], T.PI[:], T.M[:, h:h + 1], None, A.mult), ["pi", "m0", "m1"])
    vop("none", lambda: V.memset(T.HF[:, R + O:2 * HW:HW], OFF))
    vop("none", lambda: V.memset(T.HF[:, 2 * HW + R + O:4 * HW:HW], 0.0))
    vop("pt", lambda: V.transpose(T.PT[:], T.PZ[:]), ["pz"])
    for h in range(2):
        vop("of", lambda h=h: V.tensor_tensor(T.OF[:, h:64:2], T.PT[:, h:4:2, 0, :], T.PT[:, h:4:2, 1, :], A.add), ["pt"])
    vop("x0", lambda: V.tensor_copy(T.X1[:, XC[0]:XC[1]], T.XI[:, XC[0]:XC[1]]), [("dx0", 16)])
    vop("o16", lambda: V.tensor_copy(T.O16[:], T.OF[:]), ["of"])
    for c in (-2, -3):
        a, n = spans([], far)[c]
        vop("xs%d" % c, lambda a=a, n=n: V.tensor_copy(T.SB[:, a:a + n], T.XI[:, 0:S].indirect(T.SR16[:, a // 16:(a + n) // 16])), [("dx1", 16), "sr16"])
        send(0, T.SB, 0, T.X1, S, c, "xs%d" % c)
    vop("gr", lambda: V.tensor_copy(T.GT[:, 512:1024], T.CX[:, 0:R].indirect(T.O16[:, 32:64])), [("dcr", 32), "o16"])
    for c in range(2):
        dma("S", T.LS16[:, (6 + c) * 32:(7 + c) * 32], T.GT[c:128:16, 512:1024], "dwr", ["gr"])
    vop("x1", lambda: V.tensor_copy(T.X1[:, XC[1]:XC[2]], T.XI[:, XC[1]:XC[2]]))
    vop("lr", lambda: V.tensor_copy(T.L16[:, 0:224], T.RAW[:]), [("dreac", 16)])
    vop("gs", lambda: V.tensor_copy(T.GT[:, 0:512], T.CW[:, 0:S].indirect(T.O16[:, 0:32])), [("dcs", 96)])
    for c in range(6):
        dma("Y", T.LS16[:, c * 32:(c + 1) * 32], T.GT[c:128:16, 0:512], "dws", ["gs"])
    for c in range(len(CS)):
        a, n = spans(CS, far)[c]
        add("G", "ll", lambda a=a // 16, n=n // 16: g.affine_select(T.L16[:, 224 + 6 * a:224 + 6 * (a + n)], T.RAC[:, :, a:a + n],
                                                                    [[0, 6 * n]], A.is_equal, 0.0, 0, 0), [("dlist", 32)])

    for r in range(4):
        add("P", "km%d" % r, lambda r=r: P.matmul(T.ACC[:, r * 512:r * 512 + O], T.SEL[0:32, r * 128:(r + 1) * 128], T.RB[0:32, :], True, True), ["sel", "rb"])
    ks = len(ops["S"]) - 2
    for r in range(4):
        add("S", "k%d" % r, lambda r=r: Sc.activation(T.K[:, r * O:(r + 1) * O], T.ACC[:, r * 512:r * 512 + O], F.Identity, scale=1.0 / 1024), ["km%d" % r])
    add("S", "ks", lambda: Sc.activation(T.KS[:], T.K[:, 0:R].indirect(T.SR16[:, 32:60]), F.Identity), ["k3", "sr16"])
    add("S", "co", lambda: Sc.activation(T.CO[:], T.Z[:], F.Identity, bias=OFF), ["z"])
    add("S", "idf", lambda: Sc.activation(T.IDF[:], PLUS, F.Identity), ["id0"])
    ops["S"][ks:] = ops["S"][ks + 2:] + ops["S"][ks:ks + 2]

    def last(e):
        return [o[0] for o in ops[e] if o[3] is None][-1]

    def phase(kind, step, key):
        ph = "%s%d" % (kind, step)
        rnd = 4 * step + "ABCD".index(kind)
        rx = kind in "AC"
        sp = spans(CR if rx else CS, far)
        planes = {"A": 1, "B": 4, "C": 2, "D": 6}[kind]
        X = T.X1 if step == 0 else T.X2
        XS = T.SB if step == 0 else T.XS2
        h0, f0, e0 = step * HW, (2 + step) * HW, step * (S + O)
        hs, es, fs = (1 + 3 * step) * O, (2 + 3 * step) * O, (3 + 3 * step) * O
        win = {"A": X[:, 0:S + O], "B": T.HF[:, h0:h0 + R + O + 1], "C": T.E[:, e0:e0 + S + O], "D": T.HF[:, f0:f0 + R + O + 1]}[kind]
        gate = [last("V"), last("S"), ("arr%d" % rnd, arrive)] + {0: [("dwr", 32)], 1: [("dws", 96), "ll"]}.get(rnd, [])
        cl = {e: calls(t) for e, t in zip("VS", ORDER[key])}
        maker, stores = {}, []

        def place(p, c):
            a, n = sp[c]
            return p * O + a if c < 0 else p * R + a if rx else 6 * a + p * n

        def src(p, c, n):
            b = 32 * (p + (6 if rx else 0)) + sp[c][0] // 16 if c < 0 else place(p, c) // 16 + (0 if rx else 224)
            return win.indirect((T.LS16 if c < 0 else T.L16)[:, b:b + n // 16])

        def plane(p, c, n):
            return (T.PS if c < 0 else T.PL)[:, place(p, c):place(p, c) + n]

        def bank(c, n):
            b = (BANKS_A[c] if kind == "A" else c + 1) if c >= 0 else 7 if c == -3 else 0
            return T.ACC[:, b * 512:b * 512 + n]

        def own(buf, base, sbuf, s0, c, n):
            a = sp[c][0] + (s0 if c < 0 else base)
            return (sbuf if c < 0 else buf)[:, a:a + n]

        def col(buf, c, n):
            return own(buf, O, buf, 0, c, n)

        def make(e, w, ps, cs):
            c, n = cs[0], sum(sp[k][1] for k in cs)
            if w == "g":
                o, i = plane(ps[0], c, n * len(ps)), src(ps[0], c, n * len(ps))
                if kind == "B":
                    if e == "V":
                        return lambda: V.tensor_scalar(o, i, OFF + 3, OFF + 3, A.min, A.subtract)
                    return lambda: Sc.activation(o, i, F.Relu, bias=OFF + 3, scale=-1.0)
                if kind == "C":
                    if e == "V":
                        return lambda: V.tensor_scalar(o, i, 12.0, OFF / BIG, A.is_lt, A.add)
                    return lambda: Sc.activation(o, i, F.Relu, bias=12.0, scale=-1.0)
                return (lambda: V.tensor_copy(o, i)) if e == "V" else (lambda: Sc.activation(o, i, F.Identity))
            new = T.X2 if step == 0 else T.YB
            if w == "r":
                p, run = ps[0], own(T.RUN, 0, None, 0, c, n)
                o, i = own(new, 0, None, 0, c, n) if p == 5 else run, own(X, 0, None, 0, c, n) if p == 0 else run
                return lambda: V.tensor_tensor(o, src(p, c, n), i, A.subtract if p in (0, 4) else A.add)
            if w == "e":
                if kind == "C":
                    o = own(T.HF, f0, T.SB, fs, c, n)
                    if e == "V":
                        return lambda: V.tensor_scalar(o, bank(c, n), 0.0, 3.0, A.max, A.min)
                    return lambda: Sc.activation(o, bank(c, n), F.Relu)
                o = own(T.E, e0, T.SB, es, c, n) if kind == "B" else own(new, 0, T.XS2, 0, c, n)
                if e == "V":
                    return lambda: V.tensor_tensor(o, bank(c, n), own(X, 0, XS, 0, c, n), A.add)
                return lambda: Sc.activation(o, bank(c, n), F.Identity)
            if w == "u":
                return lambda: V.tensor_tensor(col(T.U, c, n), src(1, c, n), own(T.K, 0, T.KS, 0, c, n), A.mult)
            if w in "pq":
                return lambda: V.tensor_tensor(col(T.PP, c, n), bank(c, n) if w == "p" else src(0, c, n), col(T.U, c, n), A.mult)
            if w == "a":
                return lambda: Sc.activation(col(T.A1, c, n), src(0, c, n), F.Identity)
            o = own(T.HF, h0, T.SB, hs, c, n)
            shift = OFF - 1023.0 / 2048
            if e == "V":
                return lambda: V.tensor_scalar(o, col(T.PP, c, n), 3.5, shift, A.min, A.add)
            return lambda: Sc.activation(o, col(T.PP, c, n), F.Identity, bias=shift)

        due, by, reader = [], {}, {}
        for e in "VS":
            t = 0
            for w, ps, cs, word in cl[e]:
                t += 60 + sum(sp[c][1] for c in cs) * (1.5 * len(ps) if ps else 1)
                for c in cs:
                    for p in ps or [0]:
                        maker[("p" if w == "q" else w, p, c)] = ph + word
                        if w in "ga":
                            due.append((t, p, c))
                            by[(p, c)] = e
                    if w == "e":
                        reader[c] = e
                if w == "e" or (w, ps) == ("r", [5]):
                    stores.append((t, e, ph + word, sp[cs[0]][0], sum(sp[c][1] for c in cs)))
        terms = {}
        due.sort()
        if kind == "D":
            at = len([d for d in due if d[2] < 0])
            due[at:at] = [(0, None, c) for c in sorted(reader) if c >= 0]
        for _, p, c in due:
            n = sp[c][1]
            if c not in terms:
                terms[c] = []
                if kind == "C":
                    terms[c].append((PLUS, own(T.HF, h0, T.SB, hs, c, n)))
                    if by[(0, c)] == "S":
                        terms[c].append((MINUS, T.CO[:, 0:n]))
                elif reader.get(c) == "S" and kind != "B":
                    terms[c].append((PLUS if step == 0 else T.IDF[:], own(X, 0, None, 0, c, n)))
                for i, (lhs, rhs) in enumerate(terms[c]):
                    add("P", "%st%d_%d" % (ph, i, c), lambda c=c, n=n, lhs=lhs, rhs=rhs, i=i: P.matmul(bank(c, n), lhs, rhs, i == 0, False), gate[:2] + ["id2"])
            if p is None:
                continue
            if kind == "A":
                lhs, rhs, dep = PLUS, col(T.A1, c, n), maker[("a", p, c)]
            else:
                rhs, dep = plane(p, c, n), maker[("g", p, c)]
                lhs = VETO if kind == "C" else MINUS if (by[(p, c)] == "V" if kind == "B" else p < 4) else PLUS
            first = not terms[c] and (kind, reader.get(c)) != ("B", "S")
            terms[c].append(p)
            maker[("m", p, c)] = "%sm%d_%d" % (ph, p, c)
            free = [maker[("p", 0, -2)]] if kind == "A" and c >= 0 and BANKS_A[c] == 0 else []
            add("P", maker[("m", p, c)], lambda c=c, n=n, lhs=lhs, rhs=rhs, a=first, z=sum(isinstance(v, int) for v in terms[c]) == planes:
                P.matmul(bank(c, n), lhs, rhs, a, z), [dep, "id2"] + free)
            if (kind, c) == ("A", -3):
                for k in range(2):
                    add("P", "%sx%d" % (ph, k), lambda k=k: P.matmul(T.ACC[:, (k + 1) * 512:(k + 2) * 512], PLUS if step == 0 else T.IDF[:],
                                                                      X[:, k * 512:(k + 1) * 512], True, False))
        for e in "VS":
            for w, ps, cs, word in cl[e]:
                need = {"e": [("m", p) for p in range(planes)], "p": [("m", 0), ("u", 1)], "q": [("u", 1)], "h": [("p", 0)],
                        "r": [("r", p - 1) for p in ps if p]}.get(w, [])
                add(e, ph + word, make(e, w, ps, cs), gate + [maker[d + (c,)] for d in need for c in cs])
        for c in SEND.values():
            out = maker.get(("h" if kind == "A" else "e", 0, c))
            if out is not None:
                src_, s0, dst, d0 = {"A": (T.SB, hs, T.HF, h0 + R), "B": (T.SB, es, T.E, e0 + S), "C": (T.SB, fs, T.HF, f0 + R), "D": (T.XS2, 0, T.X2, S)}[kind]
                send(rnd + 1, src_, s0, dst, d0, c, out)
        return stores

    for step in range(2):
        phase("A", step, "A")
        phase("B", step, "B")
        phase("C", step, "C")
        stores = phase("D", step, "D" if step == 0 else "Z")
    for i, (_, e, name, a, n) in enumerate(sorted(stores)):
        dma("S" if name == last("S") else "Y", T.y[:, a:a + n], T.YB[:, a:a + n], "stored", [name])

    total = {}
    for e in "VSPG":
        n = 0
        for name, _, _, sem in ops[e]:
            if sem is None:
                n += 1
                where[name] = ("c" + e, n)
        total[e] = n
    for e in queue:
        got = {}
        for name, fn, deps, sem in ops[e]:
            want = {}
            for d in deps:
                s, v = where[d] if d in where else d
                want[s] = max(want.get(s, 0), v)
            for s, v in want.items():
                if got.get(s, 0) < v:
                    queue[e].wait_ge(T.sem[s], v)
                    got[s] = v
            ins = fn()
            if sem is None:
                ins.then_inc(T.sem["c" + e], 1)
            elif sem != "none":
                ins.then_inc(T.sem[sem], 16)
    for e in "VSPG":
        g.wait_ge(T.sem["c" + e], total[e])
    g.wait_ge(T.sem.sent, 8 * sent)
    Y.wait_ge(T.sem.stored, 16 * len(stores))
